import numpy as np, ml_dtypes
CORES = [14,30,46,142,158,174,270,286,302,398,414,430]
N = 12
R, C = 8, 128
def setup_inputs(rng):
    return {"x": rng.standard_normal((N, 128, C), dtype=np.float32).astype(ml_dtypes.bfloat16), "u": rng.standard_normal((N, R, 128), dtype=np.float32).astype(ml_dtypes.bfloat16), "v": rng.standard_normal((N, R, C), dtype=np.float32).astype(ml_dtypes.bfloat16)}
def setup_inputs_big(rng):
    d = setup_inputs(rng)
    for k in ("u", "v"): d[k] = (d[k].astype(np.float32) * 1024.0).astype(d[k].dtype)
    for k in ("x",): d[k] = (d[k].astype(np.float32) * 1024.0 ** 2).astype(d[k].dtype)
    return d
def setup_inputs_small(rng):
    d = setup_inputs(rng)
    for k in ("u", "v"): d[k] = (d[k].astype(np.float32) * (1 / 1024.0)).astype(d[k].dtype)
    for k in ("x",): d[k] = (d[k].astype(np.float32) * (1 / 1024.0 ** 2)).astype(d[k].dtype)
    return d
def setup_inputs_apart(rng):
    d = setup_inputs(rng)
    f = (10.0 ** rng.permutation(np.linspace(-1.5, 1.5, N))).astype(np.float32).reshape(N, 1, 1)
    for k in ("u", "v"): d[k] = (d[k].astype(np.float32) * f).astype(d[k].dtype)
    for k in ("x",): d[k] = (d[k].astype(np.float32) * f * f).astype(d[k].dtype)
    return d
def reference(x, u, v):
    X, U, V = x.astype(np.float64), u.astype(np.float64), v.astype(np.float64)
    s = V.sum(axis=0)
    return {"y": np.stack([X[r] + U[r].T @ s for r in range(N)]).astype(ml_dtypes.bfloat16 if x.dtype != np.float64 else np.float64)}

@@ -1,0 +1,78 @@
+from concourse.bass import DstId, RemoteDMATransfer
+from concourse.mybir import AluOpType
+
+R, C = 8, 128
+PIECES = 6
+
+SCRATCH = {
+    "gath": ("dram", [PIECES + 1, 128, 8], "bfloat16"),
+    "usb": ("sbuf", [128, C], "bfloat16"),
+    "gsb": ("sbuf", [128, C], "bfloat16"),
+    "osb": ("sbuf", [128, C], "bfloat16"),
+    "xsb": ("sbuf", [128, C], "bfloat16"),
+    "ysb": ("sbuf", [128, C], "bfloat16"),
+    "acc": ("psum", [128, C], "float32"),
+}
+SEMAPHORES = ["ld_v", "ld_ua", "ld_ub", "ld_x", "ld_g", "ld_o", "arr1", "arr2", "sent", "mm", "add", "st"]
+
+
+def rank_program(g, core, T, topo):
+    if T.rank_of(core) is None:
+        return
+    S = T.sem
+    my_rack = topo.rack(topo.host(core))
+    rack = [c for c in T.cores if topo.rack(topo.host(c)) == my_rack]
+    peers = [c for c in rack if c != core and topo.same_plane(core, c) and topo.may_write(core, c)]
+    far = [c for c in T.cores if topo.rack(topo.host(c)) != my_rack and topo.may_write(core, c)
+           and topo.chip(c) == topo.chip(core)]
+    assert len(rack) == PIECES and len(peers) == PIECES - 1 and len(far) == 1
+    me = rack.index(core)
+    peers = [rack[(me + k) % PIECES] for k in range(1, PIECES)]
+    usable = topo.mask(core, far[0])
+    for d in peers:
+        usable &= topo.mask(core, d)
+    eng = usable & -usable
+    n_eng = 1
+
+    def dst(d):
+        rid, pid = topo.addr(d, core)
+        return DstId(rid=rid, pnc=pid)
+
+    g.sync.dma_start(T.gath[me], T.v[:]).then_inc(S.ld_v, 16)
+    for j in range(PIECES):
+        q, sem = (g.scalar, S.ld_ub) if j % 2 == 0 else (g.sync, S.ld_ua)
+        q.dma_start(T.usb[j * R:(j + 1) * R, :], T.u[:]).then_inc(sem, 16)
+    g.scalar.dma_start(T.xsb[:, :], T.x[:]).then_inc(S.ld_x, 16)
+
+    g.wait_ge(S.ld_v, 16)
+    g.remote_dma_fused([RemoteDMATransfer(
+        dst_ids=[dst(d) for d in peers], dma_engine_mask=eng, remote_sem=S.arr1,
+        srcs=[T.gath[me]], dsts=[T.gath[me] for _ in peers], alu_op=0)], local_sem=S.sent)
+
+    g.wait_ge(S.arr1, n_eng * len(peers))
+    g.remote_dma_fused([RemoteDMATransfer(
+        dst_ids=[dst(far[0])], dma_engine_mask=eng, remote_sem=S.arr2,
+        srcs=[T.gath[j] for j in range(PIECES)], dsts=[T.gath[PIECES]], alu_op=1)], local_sem=S.sent)
+
+    g.scalar.wait_ge(S.ld_v, 16)
+    g.scalar.wait_ge(S.arr1, n_eng * len(peers))
+    g.scalar.dma_start(T.gsb[0:PIECES * R, :], T.gath[0:PIECES]).then_inc(S.ld_g, 16)
+
+    g.sync.wait_ge(S.arr2, n_eng)
+    g.sync.dma_start(T.osb[0:R, :], T.gath[PIECES]).then_inc(S.ld_o, 16)
+
+    g.tensor.wait_ge(S.ld_ua, 16 * (PIECES // 2))
+    g.tensor.wait_ge(S.ld_ub, 16 * (PIECES - PIECES // 2))
+    g.tensor.wait_ge(S.ld_g, 16)
+    g.tensor.matmul(T.acc[:, :], T.usb[0:PIECES * R, :], T.gsb[0:PIECES * R, :], start=True, stop=False).then_inc(S.mm, 1)
+    g.tensor.wait_ge(S.ld_o, 16)
+    g.tensor.matmul(T.acc[:, :], T.usb[0:R, :], T.osb[0:R, :], start=False, stop=True).then_inc(S.mm, 1)
+
+    g.vector.wait_ge(S.ld_x, 16)
+    g.vector.wait_ge(S.mm, 2)
+    g.vector.tensor_tensor(T.ysb[:, :], T.acc[:, :], T.xsb[:, :], AluOpType.add).then_inc(S.add, 1)
+    g.sync.wait_ge(S.add, 1)
+    g.sync.dma_start(T.y[:], T.ysb[:, :]).then_inc(S.st, 16)
+    g.sync.wait_ge(S.st, 16)
+
+    g.wait_ge(S.sent, 2 * n_eng)

@@ -2,10 +2,10 @@ from concourse.bass import DstId, RemoteDMATransfer
 from concourse.mybir import AluOpType
 
 R, C = 8, 128
-PIECES = 6
+DIRECT = 9
 
 SCRATCH = {
-    "gath": ("dram", [PIECES + 1, 128, 8], "bfloat16"),
+    "gath": ("dram", [DIRECT + 1, 128, 8], "bfloat16"),
     "usb": ("sbuf", [128, C], "bfloat16"),
     "gsb": ("sbuf", [128, C], "bfloat16"),
     "osb": ("sbuf", [128, C], "bfloat16"),
@@ -13,58 +13,86 @@ SCRATCH = {
     "ysb": ("sbuf", [128, C], "bfloat16"),
     "acc": ("psum", [128, C], "float32"),
 }
-SEMAPHORES = ["ld_v", "ld_ua", "ld_ub", "ld_x", "ld_g", "ld_o", "arr1", "arr2", "sent", "mm", "add", "st"]
+SEMAPHORES = ["ld_v", "ld_ua", "ld_ub", "ld_x", "ld_g", "ld_o", "arr1", "arrn", "arr2", "sent", "mm", "add", "st"]
 
 
 def rank_program(g, core, T, topo):
     if T.rank_of(core) is None:
         return
     S = T.sem
-    my_rack = topo.rack(topo.host(core))
-    rack = [c for c in T.cores if topo.rack(topo.host(c)) == my_rack]
-    peers = [c for c in rack if c != core and topo.same_plane(core, c) and topo.may_write(core, c)]
-    far = [c for c in T.cores if topo.rack(topo.host(c)) != my_rack and topo.may_write(core, c)
-           and topo.chip(c) == topo.chip(core)]
-    assert len(rack) == PIECES and len(peers) == PIECES - 1 and len(far) == 1
-    me = rack.index(core)
-    peers = [rack[(me + k) % PIECES] for k in range(1, PIECES)]
-    usable = topo.mask(core, far[0])
-    for d in peers:
-        usable &= topo.mask(core, d)
-    eng = usable & -usable
-    n_eng = 1
+
+    def rack_of(c):
+        return topo.rack(topo.host(c))
+
+    def partner(c):
+        p = [d for d in T.cores if rack_of(d) != rack_of(c) and topo.may_write(c, d) and topo.chip(d) == topo.chip(c)]
+        assert len(p) == 1
+        return p[0]
+
+    def slot(at, owner):
+        return [c for c in T.cores if c == at or topo.may_write(c, at)].index(owner)
 
     def dst(d):
         rid, pid = topo.addr(d, core)
         return DstId(rid=rid, pnc=pid)
 
-    g.sync.dma_start(T.gath[me], T.v[:]).then_inc(S.ld_v, 16)
-    for j in range(PIECES):
-        q, sem = (g.scalar, S.ld_ub) if j % 2 == 0 else (g.sync, S.ld_ua)
-        q.dma_start(T.usb[j * R:(j + 1) * R, :], T.u[:]).then_inc(sem, 16)
+    reach = [c for c in T.cores if c != core and topo.may_write(core, c)]
+    urgent = [c for c in reach if rack_of(c) == rack_of(core) and not topo.may_write(core, partner(c))]
+    cabled = [c for c in reach if rack_of(c) != rack_of(core)]
+    near = [c for c in reach if c not in urgent and c not in cabled]
+    far = partner(core)
+    relayed = [c for c in T.cores if rack_of(c) == rack_of(core) and not topo.may_write(c, far)]
+    assert len(reach) == DIRECT - 1 and len(urgent) == 3 and len(relayed) == 3 and len(cabled) == 3 and len(near) == 2
+    k0 = T.rank_of(core) % len(urgent)
+    urgent = urgent[k0:] + urgent[:k0]
+
+    usable = topo.mask(core, far)
+    for d in reach:
+        usable &= topo.mask(core, d)
+    engines = [1 << i for i in range(16) if (usable >> i) & 1][:4]
+    assert len(engines) == 4
+    four = engines[0] | engines[1] | engines[2] | engines[3]
+    mine = T.gath[slot(core, core)]
+
+    n_a = n_b = 0
+    g.sync.dma_start(mine, T.v[:]).then_inc(S.ld_v, 16)
+    for j in range(DIRECT):
+        if j % 2 == 0:
+            g.scalar.dma_start(T.usb[j * R:(j + 1) * R, :], T.u[:]).then_inc(S.ld_ub, 16)
+            n_b += 1
+        else:
+            g.sync.dma_start(T.usb[j * R:(j + 1) * R, :], T.u[:]).then_inc(S.ld_ua, 16)
+            n_a += 1
     g.scalar.dma_start(T.xsb[:, :], T.x[:]).then_inc(S.ld_x, 16)
 
     g.wait_ge(S.ld_v, 16)
     g.remote_dma_fused([RemoteDMATransfer(
-        dst_ids=[dst(d) for d in peers], dma_engine_mask=eng, remote_sem=S.arr1,
-        srcs=[T.gath[me]], dsts=[T.gath[me] for _ in peers], alu_op=0)], local_sem=S.sent)
+        dst_ids=[dst(d) for d in urgent], dma_engine_mask=engines[0], remote_sem=S.arr1,
+        srcs=[mine], dsts=[T.gath[slot(d, core)] for d in urgent], alu_op=0)], local_sem=S.sent)
 
-    g.wait_ge(S.arr1, n_eng * len(peers))
+    groups = [[cabled[0], near[0]], [cabled[1], near[1]], [cabled[2]]]
     g.remote_dma_fused([RemoteDMATransfer(
-        dst_ids=[dst(far[0])], dma_engine_mask=eng, remote_sem=S.arr2,
-        srcs=[T.gath[j] for j in range(PIECES)], dsts=[T.gath[PIECES]], alu_op=1)], local_sem=S.sent)
+        dst_ids=[dst(d) for d in grp], dma_engine_mask=engines[1 + i], remote_sem=S.arrn,
+        srcs=[mine], dsts=[T.gath[slot(d, core)] for d in grp], alu_op=0) for i, grp in enumerate(groups)],
+        local_sem=S.sent)
+
+    g.wait_ge(S.arr1, len(relayed))
+    g.remote_dma_fused([RemoteDMATransfer(
+        dst_ids=[dst(far)], dma_engine_mask=four, remote_sem=S.arr2,
+        srcs=[T.gath[slot(core, c)] for c in relayed], dsts=[T.gath[DIRECT]], alu_op=1)], local_sem=S.sent)
 
     g.scalar.wait_ge(S.ld_v, 16)
-    g.scalar.wait_ge(S.arr1, n_eng * len(peers))
-    g.scalar.dma_start(T.gsb[0:PIECES * R, :], T.gath[0:PIECES]).then_inc(S.ld_g, 16)
+    g.scalar.wait_ge(S.arr1, len(relayed))
+    g.scalar.wait_ge(S.arrn, len(cabled) + len(near))
+    g.scalar.dma_start(T.gsb[0:DIRECT * R, :], T.gath[0:DIRECT]).then_inc(S.ld_g, 16)
 
-    g.sync.wait_ge(S.arr2, n_eng)
-    g.sync.dma_start(T.osb[0:R, :], T.gath[PIECES]).then_inc(S.ld_o, 16)
+    g.sync.wait_ge(S.arr2, 4)
+    g.sync.dma_start(T.osb[0:R, :], T.gath[DIRECT]).then_inc(S.ld_o, 16)
 
-    g.tensor.wait_ge(S.ld_ua, 16 * (PIECES // 2))
-    g.tensor.wait_ge(S.ld_ub, 16 * (PIECES - PIECES // 2))
+    g.tensor.wait_ge(S.ld_ua, 16 * n_a)
+    g.tensor.wait_ge(S.ld_ub, 16 * n_b)
     g.tensor.wait_ge(S.ld_g, 16)
-    g.tensor.matmul(T.acc[:, :], T.usb[0:PIECES * R, :], T.gsb[0:PIECES * R, :], start=True, stop=False).then_inc(S.mm, 1)
+    g.tensor.matmul(T.acc[:, :], T.usb[0:DIRECT * R, :], T.gsb[0:DIRECT * R, :], start=True, stop=False).then_inc(S.mm, 1)
     g.tensor.wait_ge(S.ld_o, 16)
     g.tensor.matmul(T.acc[:, :], T.usb[0:R, :], T.osb[0:R, :], start=False, stop=True).then_inc(S.mm, 1)
 
@@ -75,4 +103,4 @@ def rank_program(g, core, T, topo):
     g.sync.dma_start(T.y[:], T.ysb[:, :]).then_inc(S.st, 16)
     g.sync.wait_ge(S.st, 16)
 
-    g.wait_ge(S.sent, 2 * n_eng)
+    g.wait_ge(S.sent, 1 + len(groups) + 4)

from concourse.bass import DstId, RemoteDMATransfer
from concourse.mybir import AluOpType

R, C = 8, 128
DIRECT = 9

SCRATCH = {
    "gath": ("dram", [DIRECT + 1, 128, 8], "bfloat16"),
    "usb": ("sbuf", [128, C], "bfloat16"),
    "gsb": ("sbuf", [128, C], "bfloat16"),
    "osb": ("sbuf", [128, C], "bfloat16"),
    "xsb": ("sbuf", [128, C], "bfloat16"),
    "ysb": ("sbuf", [128, C], "bfloat16"),
    "acc": ("psum", [128, C], "float32"),
}
SEMAPHORES = ["ld_v", "ld_ua", "ld_ub", "ld_x", "ld_g", "ld_o", "arr1", "arrn", "arr2", "sent", "mm", "add", "st"]


def rank_program(g, core, T, topo):
    if T.rank_of(core) is None:
        return
    S = T.sem

    def rack_of(c):
        return topo.rack(topo.host(c))

    def partner(c):
        p = [d for d in T.cores if rack_of(d) != rack_of(c) and topo.may_write(c, d) and topo.chip(d) == topo.chip(c)]
        assert len(p) == 1
        return p[0]

    def slot(at, owner):
        return [c for c in T.cores if c == at or topo.may_write(c, at)].index(owner)

    def dst(d):
        rid, pid = topo.addr(d, core)
        return DstId(rid=rid, pnc=pid)

    reach = [c for c in T.cores if c != core and topo.may_write(core, c)]
    urgent = [c for c in reach if rack_of(c) == rack_of(core) and not topo.may_write(core, partner(c))]
    cabled = [c for c in reach if rack_of(c) != rack_of(core)]
    near = [c for c in reach if c not in urgent and c not in cabled]
    far = partner(core)
    relayed = [c for c in T.cores if rack_of(c) == rack_of(core) and not topo.may_write(c, far)]
    assert len(reach) == DIRECT - 1 and len(urgent) == 3 and len(relayed) == 3 and len(cabled) == 3 and len(near) == 2
    k0 = T.rank_of(core) % len(urgent)
    urgent = urgent[k0:] + urgent[:k0]

    usable = topo.mask(core, far)
    for d in reach:
        usable &= topo.mask(core, d)
    engines = [1 << i for i in range(16) if (usable >> i) & 1][:4]
    assert len(engines) == 4
    four = engines[0] | engines[1] | engines[2] | engines[3]
    mine = T.gath[slot(core, core)]

    n_a = n_b = 0
    g.sync.dma_start(mine, T.v[:]).then_inc(S.ld_v, 16)
    for j in range(DIRECT):
        if j % 2 == 0:
            g.scalar.dma_start(T.usb[j * R:(j + 1) * R, :], T.u[:]).then_inc(S.ld_ub, 16)
            n_b += 1
        else:
            g.sync.dma_start(T.usb[j * R:(j + 1) * R, :], T.u[:]).then_inc(S.ld_ua, 16)
            n_a += 1
    g.scalar.dma_start(T.xsb[:, :], T.x[:]).then_inc(S.ld_x, 16)

    g.wait_ge(S.ld_v, 16)
    g.remote_dma_fused([RemoteDMATransfer(
        dst_ids=[dst(d) for d in urgent], dma_engine_mask=engines[0], remote_sem=S.arr1,
        srcs=[mine], dsts=[T.gath[slot(d, core)] for d in urgent], alu_op=0)], local_sem=S.sent)

    groups = [[cabled[0], near[0]], [cabled[1], near[1]], [cabled[2]]]
    g.remote_dma_fused([RemoteDMATransfer(
        dst_ids=[dst(d) for d in grp], dma_engine_mask=engines[1 + i], remote_sem=S.arrn,
        srcs=[mine], dsts=[T.gath[slot(d, core)] for d in grp], alu_op=0) for i, grp in enumerate(groups)],
        local_sem=S.sent)

    g.wait_ge(S.arr1, len(relayed))
    g.remote_dma_fused([RemoteDMATransfer(
        dst_ids=[dst(far)], dma_engine_mask=four, remote_sem=S.arr2,
        srcs=[T.gath[slot(core, c)] for c in relayed], dsts=[T.gath[DIRECT]], alu_op=1)], local_sem=S.sent)

    g.scalar.wait_ge(S.ld_v, 16)
    g.scalar.wait_ge(S.arr1, len(relayed))
    g.scalar.wait_ge(S.arrn, len(cabled) + len(near))
    g.scalar.dma_start(T.gsb[0:DIRECT * R, :], T.gath[0:DIRECT]).then_inc(S.ld_g, 16)

    g.sync.wait_ge(S.arr2, 4)
    g.sync.dma_start(T.osb[0:R, :], T.gath[DIRECT]).then_inc(S.ld_o, 16)

    g.tensor.wait_ge(S.ld_ua, 16 * n_a)
    g.tensor.wait_ge(S.ld_ub, 16 * n_b)
    g.tensor.wait_ge(S.ld_g, 16)
    g.tensor.matmul(T.acc[:, :], T.usb[0:DIRECT * R, :], T.gsb[0:DIRECT * R, :], start=True, stop=False).then_inc(S.mm, 1)
    g.tensor.wait_ge(S.ld_o, 16)
    g.tensor.matmul(T.acc[:, :], T.usb[0:R, :], T.osb[0:R, :], start=False, stop=True).then_inc(S.mm, 1)

    g.vector.wait_ge(S.ld_x, 16)
    g.vector.wait_ge(S.mm, 2)
    g.vector.tensor_tensor(T.ysb[:, :], T.acc[:, :], T.xsb[:, :], AluOpType.add).then_inc(S.add, 1)
    g.sync.wait_ge(S.add, 1)
    g.sync.dma_start(T.y[:], T.ysb[:, :]).then_inc(S.st, 16)
    g.sync.wait_ge(S.st, 16)

    g.wait_ge(S.sent, 1 + len(groups) + 4)
